import numpy as np
import ml_dtypes


def mxq(x, axis, fmt="e4m3"):
    dtype, down = {"e4m3": (ml_dtypes.float8_e4m3fn, 7), "e5m2": (ml_dtypes.float8_e5m2, 14)}[fmt]
    v = np.moveaxis(np.asarray(x, np.float32).astype(ml_dtypes.bfloat16).astype(np.float64), axis, -1)
    blocks = v.reshape(v.shape[:-1] + (-1, 32))
    amax = np.abs(blocks).max(-1, keepdims=True)
    byte = np.maximum(np.where(amax > 0, np.frexp(amax)[1] - 1 + 127, 0) - down, 1)
    scale = np.exp2(byte - 127.0)
    codes = (blocks / scale).astype(np.float32).astype(dtype).astype(np.float64)
    return np.moveaxis((codes * scale).reshape(v.shape), -1, axis)


WIDE = False


def mx_kscale(k):
    if not WIDE:
        return np.ones(k)
    levels = np.array([10, -10, 5, -5, 0])
    if k % 512:
        return np.exp2(np.random.permutation(np.resize(levels, k // 32))).repeat(32)
    a = np.empty((k // 512, 16))
    for p in range(k // 512):
        a[p, :8] = np.random.permutation(np.resize(levels, 8))
        for g in range(8):
            far = levels[np.abs(levels - a[p, g]) >= 10]
            a[p, g + 8] = far[np.random.randint(len(far))]
    return np.exp2(a.ravel()).repeat(32)


BF16 = ml_dtypes.bfloat16


def bf(x):
    return np.asarray(x, np.float32).astype(BF16)


def f64(x):
    return np.asarray(x).astype(np.float64)


E2M1 = np.array([0.0, 0.5, 1.0, 1.5, 2.0, 3.0, 4.0, 6.0, -0.0, -0.5, -1.0, -1.5, -2.0, -3.0, -4.0, -6.0])


def pack_weight(w, fmt):
    k, n = w.shape
    w = f64(bf(w)).reshape(k // 32, 32, n)
    amax = np.abs(w).max(1)
    if fmt == "e4m3":
        byte = np.frexp(amax)[1] - 1 + 127 - 7
    else:
        mant, ex = np.frexp(amax / 6.0)
        byte = np.where(mant > 0.5, ex, ex - 1) + 127
    byte = np.clip(np.where(amax > 0, byte, 1), 1, 254)
    scaled = (w * np.exp2(127.0 - byte)[:, None, :]).reshape(k, n).astype(np.float32)
    by_word = np.ascontiguousarray(scaled.reshape(k // 512, 128, 4, n).transpose(0, 1, 3, 2))
    if fmt == "e4m3":
        words = by_word.astype(ml_dtypes.float8_e4m3fn).view(np.uint8)
    else:
        c = by_word.astype(ml_dtypes.float4_e2m1fn).view(np.uint8) & 0xF
        words = c[..., 0::2] | (c[..., 1::2] << 4)
    return np.ascontiguousarray(words), np.ascontiguousarray(byte.astype(np.uint8).reshape(k // 512, 16, n))


def unpack_weight(words, scales, fmt):
    g, p, n, _ = words.shape
    if fmt == "e4m3":
        vals = np.ascontiguousarray(words).view(ml_dtypes.float8_e4m3fn).astype(np.float64)
    else:
        nib = np.empty((g, p, n, 4), np.uint8)
        nib[..., 0::2] = words & 0xF
        nib[..., 1::2] = words >> 4
        vals = E2M1[nib]
    vals = vals * np.repeat(np.exp2(scales.astype(np.float64) - 127.0), 8, axis=1)[..., None]
    return vals.transpose(0, 1, 3, 2).reshape(g * 512, n)
def pack4(w):
    words, scales = pack_weight(w, "e2m1")
    return words.reshape(words.shape[0], 128, -1), scales


def unpack4(words, scales):
    return unpack_weight(words.reshape(words.shape[0], 128, -1, 2), scales, "e2m1")


M, K, N = 1024, 1536, 1024


def setup_inputs():
    s = mx_kscale(K)
    spectra = bf(np.random.standard_normal((M, K)) * s)
    shift = 0.5 * np.random.standard_normal((K, N)) / np.sqrt(K) / s[:, None]
    pinv = np.random.standard_normal((K, N)) / np.sqrt(K) / s[:, None]
    base = bf(0.5 * np.random.standard_normal((K, N)) / np.sqrt(K) / s[:, None])
    eps = bf(1 + 0.1 * np.random.standard_normal(N))
    shift_words, shift_scales = pack4(shift)
    pinv_words, pinv_scales = pack_weight(pinv, "e4m3")
    return {"spectra": spectra,
            "shift_words": shift_words, "shift_scales": shift_scales,
            "pinv_words": pinv_words, "pinv_scales": pinv_scales,
            "base": base, "eps": eps}


def reference(spectra, shift_words, shift_scales, pinv_words, pinv_scales, base, eps):
    a = mxq(f64(spectra), 1, "e4m3")
    conc = np.maximum(a @ unpack_weight(pinv_words, pinv_scales, "e4m3"), 0.0)
    absorptivity = f64(eps) + (a @ unpack4(shift_words, shift_scales))
    baseline = a @ mxq(f64(base), 0, "e4m3")
    rebuilt = conc * absorptivity + baseline
    return conc, rebuilt

@@ -1,0 +1,323 @@
+from contextlib import ExitStack
+
+import concourse.mybir as mybir
+from concourse.masks import make_identity
+
+M, K, N = 1024, 1536, 1024
+FLOPS = 3 * 2 * M * K * N
+
+F32 = mybir.dt.float32
+BF16 = mybir.dt.bfloat16
+I32 = mybir.dt.int32
+U32 = mybir.dt.uint32
+U8 = mybir.dt.uint8
+FP8X4 = mybir.dt.float8_e4m3fn_x4
+FP4X4 = mybir.dt.float4_e2m1fn_x4
+ALU = mybir.AluOpType
+ACT = mybir.ActivationFunctionType
+
+P = 128
+PACK = 4
+K_PASS = P * PACK
+PASSES = K // K_PASS
+TILES = M // P
+HALF = 512
+HALVES = N // HALF
+BANKS = 8
+PINV_ROW = 4
+PIECE = 128
+PIECES = HALF // PIECE
+
+
+def schedule():
+    s = []
+    s += [("load_first", 0), ("load_eps",), ("load_first", 1), ("load_first", 2), ("load_shift", 0)]
+    s += [("table",), ("zero_shift",), ("zero_pinv",), ("ident",), ("load_shift_scales",)]
+    s += [("load_pair", 1), ("load_pinv_scales",)]
+    s += [("load_pinv", 0, g, g + 1) for g in range(PASSES)]
+    s += [("load_pair", 2), ("load_pair", 3), ("load_base", 0), ("load_base", 1)]
+    s += [("load_shift", 1), ("load_pinv", 1, 0, PASSES), ("load_base", 2)]
+    s += [("sort", 0), ("sort", 1), ("sort", 2), ("turn", 0), ("turn", 1), ("turn", 2), ("turn_eps",)]
+    s += [("copy", 0), ("copy", 1), ("quant", 0), ("copy", 2), ("quant", 1), ("quant", 2), ("copy_eps",)]
+    s += [("mm_both", "shift")]
+    s += [("sort", 3), ("sort", 4), ("sort", 5)]
+    s += [("turn", 3), ("turn", 4), ("turn", 5), ("add_eps", 0, 0), ("copy", 3), ("copy", 4), ("copy", 5)]
+    s += [("mm_both", "pinv"), ("quant", 3), ("add_eps", 1, 0), ("quant", 4), ("quant", 5)]
+    s += [("relu", 0, 0), ("relu", 1, 0), ("sort", 6), ("sort", 7), ("sort", 8), ("mult", 0, 0)]
+    pieces = [("weave", g, h, i, "act") for h in range(HALVES) for g in range(PASSES) for i in range(PIECES)]
+    woven = []
+    quantised = []
+
+    def weave(n):
+        out = pieces[len(woven) : len(woven) + n]
+        woven.extend(out)
+        return out
+
+    def quant_base():
+        if len(quantised) >= len(woven) // PIECES:
+            return []
+        h, g = divmod(len(quantised), PASSES)
+        quantised.append((g, h))
+        return [("quant_base", g, h)]
+
+    for j in range(1, 4):
+        a, b = 2 * j, 2 * j + 1
+        t = 3 * (j + 1)
+        s += [("mm", "shift", a, 0), ("mult", a - 1, 0)]
+        s += [("add_eps", a, 0), ("mm", "pinv", a, 0), ("relu", a, 0)]
+        if j < 3:
+            s += [("turn", t), ("turn", t + 1), ("turn", t + 2), ("mult", a, 0)]
+            s += [("copy", t), ("copy", t + 1), ("quant", t), ("copy", t + 2), ("quant", t + 1), ("quant", t + 2)]
+            s += weave(j - 1)
+        else:
+            s += quant_base() + weave(2) + [("mult", a, 0)]
+        s += [("mm", "shift", b, 0), ("add_eps", b, 0)]
+        if j < 2:
+            s += [("sort", t + 3), ("sort", t + 4), ("sort", t + 5)]
+        s += [("mm", "pinv", b, 0), ("relu", b, 0)] + weave(2 if j > 1 else 1)
+    for m in range(TILES):
+        s += [("store_conc", m, 0)]
+    lag = 4
+    prev = (TILES - 1, 0)
+    whole = (0, HALF)
+    for m in range(TILES):
+        s += [("mm", "shift", m, 1), ("mult",) + prev] + quant_base()
+        s += [("add_eps", m, 1), ("mm", "pinv", m, 1), ("relu", m, 1), ("store_conc", m, 1)]
+        s += weave(2 if m < lag else 3)
+        prev = (m, 1)
+        if m >= lag:
+            s += [("mm", "base", m - lag, 0) + whole, ("final", m - lag, 0) + whole, ("store_rebuilt", m - lag, 0) + whole]
+    rest = [(m, 0) + whole for m in range(TILES - lag, TILES)] + [(m, 1) + whole for m in range(TILES - 2)]
+    rest += [(TILES - 2, 1, 0, 256), (TILES - 2, 1, 256, 256)]
+    rest += [(TILES - 1, 1, 0, 256), (TILES - 1, 1, 256, 128), (TILES - 1, 1, 384, 128)]
+    for i, part in enumerate(rest):
+        s += [("mm", "base") + part]
+        if i == 0:
+            s += [("mult",) + prev]
+        s += quant_base() + [("final",) + part, ("store_rebuilt",) + part]
+    assert len(woven) == len(pieces) and len(quantised) == PASSES * HALVES
+    return s
+
+
+def tile_spectral_unmix_rebuild_s10_kernel(
+    tc, spectra, shift_words, shift_scales, pinv_words, pinv_scales, base, eps, conc_out, rebuilt_out
+):
+    nc = tc.nc
+    with ExitStack() as ctx:
+        keep = ctx.enter_context(tc.tile_pool(name="keep", bufs=1))
+        stage = ctx.enter_context(tc.tile_pool(name="stage", bufs=4))
+        psum = ctx.enter_context(tc.psum_pool(name="psum", bufs=1))
+        ctx.enter_context(tc.manual_schedule())
+
+        ident = keep.tile([P, P], F32, name="ident", align_bytes=64)
+        x_first = [keep.tile([P, 2, K_PASS], BF16, name=f"x0_{g}", align_bytes=64) for g in range(PASSES)]
+        x_pair = {j: keep.tile([P, 2, K], BF16, name=f"x{j}", align_bytes=64) for j in range(1, TILES // 2)}
+        scratch = keep.tile([P, 8], F32, name="scratch", align_bytes=64)
+        seed = keep.tile([P, 8], F32, name="seed", align_bytes=64)
+        x_sorted = {}
+        base_sb = [keep.tile([P, PACK, N], BF16, name=f"base{g}", align_bytes=64) for g in range(PASSES)]
+        shift_codes = [keep.tile([P, PASSES, 2 * HALF], U8, name=f"sw{h}", align_bytes=64) for h in range(HALVES)]
+        pinv_codes = [keep.tile([P, PASSES, HALF], U32, name=f"pw{h}", align_bytes=64) for h in range(HALVES)]
+        shift_plane = keep.tile([P, PASSES, N], U8, name="shift_plane", align_bytes=64)
+        pinv_plane = keep.tile([P, PASSES, N], U8, name="pinv_plane", align_bytes=64)
+        base_codes = keep.tile([P, PASSES, N], U32, name="base_codes", align_bytes=64)
+        base_plane = keep.tile([P, PASSES, N], U8, name="base_plane", align_bytes=64)
+        x_codes = keep.tile([P, TILES * PASSES * P], U32, name="x_codes", align_bytes=64)
+        x_plane = keep.tile([P, TILES * PASSES * P], U8, name="x_plane", align_bytes=64)
+        eps_rows = keep.tile([P, N // P], BF16, name="eps_rows", align_bytes=64)
+        eps_all = keep.tile([P, N], BF16, name="eps_all", align_bytes=64)
+        conc = {}
+        work = {}
+        for m in range(TILES):
+            for h in range(HALVES):
+                conc[m, h] = keep.tile([P, HALF], F32, name=f"conc{m}_{h}", align_bytes=64)
+                work[m, h] = keep.tile([P, HALF], F32, name=f"work{m}_{h}", align_bytes=64)
+
+        banks = {}
+        x_woven = {}
+        base_woven = {}
+        taken = []
+
+        def new_bank(key):
+            banks[key] = psum.tile([P, HALF], F32, name=f"bank{len(taken) % BANKS}")
+            taken.append(key)
+            return banks[key]
+
+        def rows(m):
+            return slice(m * P, (m + 1) * P)
+
+        def cols(h):
+            return slice(h * HALF, (h + 1) * HALF)
+
+        def load_first(g):
+            src = spectra[0 : 2 * P, g * K_PASS : (g + 1) * K_PASS].rearrange("(t p) k -> p t k", p=P)
+            nc.sync.dma_start(out=x_first[g][:], in_=src)
+
+        def load_pair(j):
+            src = spectra[2 * j * P : 2 * (j + 1) * P, :].rearrange("(t p) k -> p t k", p=P)
+            nc.sync.dma_start(out=x_pair[j][:], in_=src)
+
+        def table():
+            nc.vector.memset(seed[:], 0.0)
+            nc.scalar.activation(out=scratch[:], in_=seed[:], func=ACT.Relu)
+
+        def sort(b):
+            j, g = divmod(b, PASSES)
+            x_sorted[b] = stage.tile([P, 2, 2, P], F32, name="x_sorted", align_bytes=64)
+            if j == 0:
+                words = x_first[g][:].bitcast(F32)
+            else:
+                words = x_pair[j][:].bitcast(F32)[:, :, 2 * P * g : 2 * P * (g + 1)]
+            nc.vector.tensor_copy(out=x_sorted[b][:], in_=words.rearrange("p t (w u) -> p t u w", u=2))
+
+        def load_eps():
+            nc.scalar.dma_start(out=eps_rows[:], in_=eps.rearrange("(p c) -> p c", p=P))
+
+        def load_scales(queue, plane, scales, first_row):
+            by_row = scales.rearrange("g (q r) n -> r q g n", r=4)
+            for r in range(4):
+                queue.dma_start(out=plane[first_row + r : P : 32, :, :].bitcast(I32), in_=by_row[r].bitcast(I32))
+
+        def load_shift(h):
+            src = shift_words.rearrange("g p c -> p g c")[:, :, h * 2 * HALF : (h + 1) * 2 * HALF]
+            nc.sync.dma_start(out=shift_codes[h][:].bitcast(I32), in_=src.bitcast(I32))
+
+        def load_pinv(h, g0, g1):
+            src = pinv_words.rearrange("g p n t -> p g (n t)")[:, g0:g1, h * PACK * HALF : (h + 1) * PACK * HALF]
+            nc.sync.dma_start(out=pinv_codes[h][:, g0:g1, :].bitcast(I32), in_=src.bitcast(I32))
+
+        def load_base(g):
+            src = base[g * K_PASS : (g + 1) * K_PASS, :].rearrange("(p j) n -> p j n", j=PACK)
+            nc.sync.dma_start(out=base_sb[g][:], in_=src)
+
+        def zero(plane):
+            nc.vector.memset(plane[:].rearrange("p g n -> p (g n)").bitcast(I32), 0)
+
+        def turn(b):
+            bank = new_bank(("turn", b))
+            for t in range(2):
+                for u in range(2):
+                    out = bank[:, (2 * t + u) * P : (2 * t + u + 1) * P]
+                    nc.tensor.transpose(out, x_sorted[b][:, t, u, :], ident[:])
+
+        def copy(b):
+            woven = stage.tile([P, 2 * K_PASS], BF16, name="x_woven", align_bytes=64)
+            x_woven[b] = woven
+            nc.scalar.copy(
+                out=woven[:].bitcast(F32).rearrange("p (i r u) -> p i r u", i=2, u=2),
+                in_=banks["turn", b][:].rearrange("p (i u r) -> p i r u", i=2, u=2),
+            )
+
+        def quant(b):
+            span = slice(2 * b * P, 2 * (b + 1) * P)
+            nc.vector.quantize_mx(out=x_codes[:, span].bitcast(FP8X4), scales=x_plane[:, span], in_=x_woven[b][:])
+
+        def turn_eps():
+            bank = new_bank("eps")
+            words = eps_rows[:].bitcast(F32)
+            for c in range(4):
+                nc.tensor.transpose(bank[:, c * P : (c + 1) * P], words[:, c : c + 1].to_broadcast([P, P]), ident[:])
+
+        def copy_eps():
+            nc.scalar.copy(
+                out=eps_all[:].bitcast(F32).rearrange("p (n c) -> p n c", c=4),
+                in_=banks["eps"][:].rearrange("p (c n) -> p n c", c=4),
+            )
+
+        def weave(g, h, piece, engine):
+            if piece == 0:
+                base_woven[g, h] = stage.tile([P, HALF, PACK], BF16, name="base_woven", align_bytes=64)
+            span = slice(piece * PIECE, (piece + 1) * PIECE)
+            out = base_woven[g, h][:, span, :].rearrange("p (c i) t -> p c t i", i=4)
+            src = base_sb[g][:, :, cols(h)][:, :, span].rearrange("p t (c i) -> p c t i", i=4)
+            if engine == "act":
+                nc.scalar.copy(out=out, in_=src)
+            else:
+                nc.vector.tensor_copy(out=out, in_=src)
+
+        def quant_base(g, h):
+            nc.vector.quantize_mx(
+                out=base_codes[:, g, cols(h)].bitcast(FP8X4),
+                scales=base_plane[:, g, cols(h)],
+                in_=base_woven[g, h][:].rearrange("p n t -> p (n t)"),
+            )
+
+        def mm_both(which):
+            for g in range(PASSES):
+                for m in range(2):
+                    mm(which, m, 0, passes=[g])
+
+        def mm(which, m, h, first=0, width=HALF, passes=range(PASSES)):
+            for g in passes:
+                bank = new_bank((which, m, h, first)) if g == 0 else banks[which, m, h, first]
+                block = 2 * (PASSES * (m // 2) + g) + m % 2
+                span = slice(block * P, (block + 1) * P)
+                if which == "shift":
+                    rhs, rhs_scale = shift_codes[h][:, g, :].bitcast(FP4X4), shift_plane[:, g, cols(h)]
+                elif which == "pinv":
+                    rhs, rhs_scale = pinv_codes[h][:, g, :].bitcast(FP8X4), pinv_plane[PINV_ROW:, g, cols(h)]
+                else:
+                    part = slice(h * HALF + first, h * HALF + first + width)
+                    rhs, rhs_scale = base_codes[:, g, part].bitcast(FP8X4), base_plane[:, g, part]
+                nc.tensor.matmul_mx(
+                    out=bank[:, :width],
+                    lhsT=x_codes[:, span].bitcast(FP8X4),
+                    lhsT_scale=x_plane[:, span],
+                    rhs=rhs,
+                    rhs_scale=rhs_scale,
+                    start=(g == 0),
+                    stop=(g == PASSES - 1),
+                )
+
+        def add_eps(m, h):
+            nc.vector.tensor_tensor(out=work[m, h][:], in0=banks["shift", m, h, 0][:], in1=eps_all[:, cols(h)], op=ALU.add)
+
+        def relu(m, h):
+            nc.scalar.activation(out=conc[m, h][:], in_=banks["pinv", m, h, 0][:], func=ACT.Relu)
+
+        def mult(m, h):
+            nc.vector.tensor_tensor(out=work[m, h][:], in0=work[m, h][:], in1=conc[m, h][:], op=ALU.mult)
+
+        def final(m, h, first, width):
+            part = work[m, h][:, first : first + width]
+            nc.vector.tensor_tensor(out=part, in0=banks["base", m, h, first][:, :width], in1=part, op=ALU.add)
+
+        def store_conc(m, h):
+            nc.sync.dma_start(out=conc_out[rows(m), cols(h)], in_=conc[m, h][:])
+
+        def store_rebuilt(m, h, first, width):
+            part = slice(h * HALF + first, h * HALF + first + width)
+            nc.sync.dma_start(out=rebuilt_out[rows(m), part], in_=work[m, h][:, first : first + width])
+
+        steps = {
+            "load_first": load_first,
+            "load_pair": load_pair,
+            "table": table,
+            "sort": sort,
+            "load_eps": load_eps,
+            "zero_shift": lambda: zero(shift_plane),
+            "zero_pinv": lambda: zero(pinv_plane),
+            "ident": lambda: make_identity(nc, ident[:]),
+            "load_shift_scales": lambda: load_scales(nc.scalar, shift_plane, shift_scales, 0),
+            "load_pinv_scales": lambda: load_scales(nc.sync, pinv_plane, pinv_scales, PINV_ROW),
+            "load_shift": load_shift,
+            "load_pinv": load_pinv,
+            "load_base": load_base,
+            "turn": turn,
+            "copy": copy,
+            "quant": quant,
+            "turn_eps": turn_eps,
+            "copy_eps": copy_eps,
+            "weave": weave,
+            "quant_base": quant_base,
+            "mm": mm,
+            "mm_both": mm_both,
+            "add_eps": add_eps,
+            "relu": relu,
+            "mult": mult,
+            "final": final,
+            "store_conc": store_conc,
+            "store_rebuilt": store_rebuilt,
+        }
+        for step in schedule():
+            steps[step[0]](*step[1:])

@@ -31,22 +31,18 @@ PIECES = HALF // PIECE
 
 def schedule():
     s = []
-    s += [("load_first", 0), ("load_eps",), ("load_first", 1), ("load_first", 2), ("load_shift", 0)]
-    s += [("table",), ("zero_shift",), ("zero_pinv",), ("ident",), ("load_shift_scales",)]
-    s += [("load_pair", 1), ("load_pinv_scales",)]
-    s += [("load_pinv", 0, g, g + 1) for g in range(PASSES)]
-    s += [("load_pair", 2), ("load_pair", 3), ("load_base", 0), ("load_base", 1)]
-    s += [("load_shift", 1), ("load_pinv", 1, 0, PASSES), ("load_base", 2)]
-    s += [("sort", 0), ("sort", 1), ("sort", 2), ("turn", 0), ("turn", 1), ("turn", 2), ("turn_eps",)]
-    s += [("copy", 0), ("copy", 1), ("quant", 0), ("copy", 2), ("quant", 1), ("quant", 2), ("copy_eps",)]
-    s += [("mm_both", "shift")]
-    s += [("sort", 3), ("sort", 4), ("sort", 5)]
-    s += [("turn", 3), ("turn", 4), ("turn", 5), ("add_eps", 0, 0), ("copy", 3), ("copy", 4), ("copy", 5)]
-    s += [("mm_both", "pinv"), ("quant", 3), ("add_eps", 1, 0), ("quant", 4), ("quant", 5)]
-    s += [("relu", 0, 0), ("relu", 1, 0), ("sort", 6), ("sort", 7), ("sort", 8), ("mult", 0, 0)]
+    s += [("load_first", 0), ("load_first", 1), ("load_first", 2), ("load_shift", 0)]
+    s += [("zero_shift",), ("zero_pinv",), ("ident",), ("load_shift_scales",), ("table",), ("load_eps",), ("load_pinv_scales",)]
+    s += [("load_pair", 1), ("load_base", 0, 0)] + [("load_pinv", 0, g, g + 1) for g in range(PASSES)]
+    s += [("load_pair", 2), ("load_pair", 3), ("load_base", 1, 0), ("load_base", 2, 0)]
+    s += [("load_shift", 1), ("load_pinv", 1, 0, PASSES)] + [("load_base", g, 1) for g in range(PASSES)]
+
     pieces = [("weave", g, h, i, "act") for h in range(HALVES) for g in range(PASSES) for i in range(PIECES)]
     woven = []
     quantised = []
+    to_mult = [(m, h) for h in range(HALVES) for m in range(TILES)]
+    multiplied = []
+    whole = (0, HALF)
 
     def weave(n):
         out = pieces[len(woven) : len(woven) + n]
@@ -54,48 +50,63 @@ def schedule():
         return out
 
     def quant_base():
-        if len(quantised) >= len(woven) // PIECES:
-            return []
         h, g = divmod(len(quantised), PASSES)
         quantised.append((g, h))
+        assert len(woven) >= PIECES * len(quantised)
         return [("quant_base", g, h)]
+
+    def mult(n):
+        out = to_mult[len(multiplied) : len(multiplied) + n]
+        multiplied.extend(out)
+        return [("mult",) + tile for tile in out]
+
+    def finish(part):
+        return [("mm", "base") + part, ("final",) + part, ("store_rebuilt",) + part]
+
+    s += [("sort", 0), ("sort", 1), ("sort", 2), ("turn", 0), ("turn", 1), ("turn", 2), ("turn_eps",)]
+    s += [("copy", 0), ("copy", 1), ("quant", 0), ("copy", 2), ("quant", 1), ("quant", 2), ("copy_eps",)]
+    s += [("mm_both", "shift"), ("sort", 3), ("sort", 4), ("sort", 5)] + weave(2)
+    s += [("turn", 3), ("turn", 4), ("turn", 5), ("add_eps", 0, 0), ("add_eps", 1, 0)]
+    s += [("copy", 3), ("copy", 4, "dve"), ("copy", 5), ("mm_both", "pinv")]
+    s += [("quant", 3), ("quant", 4), ("quant", 5), ("sort", 6), ("sort", 7), ("sort", 8)]
+    s += weave(1) + [("relu", 0, 0)]
 
     for j in range(1, 4):
         a, b = 2 * j, 2 * j + 1
         t = 3 * (j + 1)
-        s += [("mm", "shift", a, 0), ("mult", a - 1, 0)]
-        s += [("add_eps", a, 0), ("mm", "pinv", a, 0), ("relu", a, 0)]
+        s += [("mm", "shift", a, 0), ("relu", a - 1, 0)] + weave(1)
+        s += mult([1,1,0][j - 1]) + [("add_eps", a, 0)] + mult([1,1,1][j - 1])
         if j < 3:
-            s += [("turn", t), ("turn", t + 1), ("turn", t + 2), ("mult", a, 0)]
-            s += [("copy", t), ("copy", t + 1), ("quant", t), ("copy", t + 2), ("quant", t + 1), ("quant", t + 2)]
-            s += weave(j - 1)
-        else:
-            s += quant_base() + weave(2) + [("mult", a, 0)]
-        s += [("mm", "shift", b, 0), ("add_eps", b, 0)]
-        if j < 2:
-            s += [("sort", t + 3), ("sort", t + 4), ("sort", t + 5)]
-        s += [("mm", "pinv", b, 0), ("relu", b, 0)] + weave(2 if j > 1 else 1)
-    for m in range(TILES):
+            s += [("turn", t), ("turn", t + 1), ("turn", t + 2), ("copy", t), ("copy", t + 1), ("copy", t + 2)]
+            s += [("quant", t)] + ([("sort", 9)] if j == 1 else []) + [("quant", t + 1), ("quant", t + 2)]
+            s += [("sort", 10), ("sort", 11)] if j == 1 else []
+        s += [("mm", "pinv", a, 0), ("mm", "shift", b, 0), ("relu", a, 0)] + weave(1 if j < 3 else 2)
+        s += [("add_eps", b, 0), ("mm", "pinv", b, 0)]
+        if j > 1:
+            s += quant_base()
+    for m in range(TILES - 1):
         s += [("store_conc", m, 0)]
-    lag = 4
+    lag = 3
     prev = (TILES - 1, 0)
-    whole = (0, HALF)
     for m in range(TILES):
-        s += [("mm", "shift", m, 1), ("mult",) + prev] + quant_base()
-        s += [("add_eps", m, 1), ("mm", "pinv", m, 1), ("relu", m, 1), ("store_conc", m, 1)]
-        s += weave(2 if m < lag else 3)
+        s += [("mm", "shift", m, 1), ("relu",) + prev, ("store_conc",) + prev]
+        s += weave([2,1,2,2,3,2,2,0][m]) + mult([1,1,1,2,1,1,1,1][m]) + [("add_eps", m, 1), ("mm", "pinv", m, 1)]
+        if m in [1,4,6,7]:
+            s += quant_base()
         prev = (m, 1)
         if m >= lag:
-            s += [("mm", "base", m - lag, 0) + whole, ("final", m - lag, 0) + whole, ("store_rebuilt", m - lag, 0) + whole]
+            s += finish((m - lag, 0) + whole)
     rest = [(m, 0) + whole for m in range(TILES - lag, TILES)] + [(m, 1) + whole for m in range(TILES - 2)]
     rest += [(TILES - 2, 1, 0, 256), (TILES - 2, 1, 256, 256)]
     rest += [(TILES - 1, 1, 0, 256), (TILES - 1, 1, 256, 128), (TILES - 1, 1, 384, 128)]
+    s += [("relu",) + prev, ("store_conc",) + prev] + weave(PIECES)
     for i, part in enumerate(rest):
-        s += [("mm", "base") + part]
-        if i == 0:
-            s += [("mult",) + prev]
-        s += quant_base() + [("final",) + part, ("store_rebuilt",) + part]
-    assert len(woven) == len(pieces) and len(quantised) == PASSES * HALVES
+        if i == 99:
+            s += quant_base()
+        s += finish(part)
+        if i in [0,2]:
+            s += mult(1)
+    assert len(woven) == len(pieces) and len(quantised) == PASSES * HALVES and len(multiplied) == 2 * TILES
     return s
 
 
@@ -115,7 +126,10 @@ def tile_spectral_unmix_rebuild_s10_kernel(
         scratch = keep.tile([P, 8], F32, name="scratch", align_bytes=64)
         seed = keep.tile([P, 8], F32, name="seed", align_bytes=64)
         x_sorted = {}
-        base_sb = [keep.tile([P, PACK, N], BF16, name=f"base{g}", align_bytes=64) for g in range(PASSES)]
+        base_sb = {}
+        for g in range(PASSES):
+            for h in range(HALVES):
+                base_sb[g, h] = keep.tile([P, PACK, HALF], BF16, name=f"base{g}_{h}", align_bytes=64)
         shift_codes = [keep.tile([P, PASSES, 2 * HALF], U8, name=f"sw{h}", align_bytes=64) for h in range(HALVES)]
         pinv_codes = [keep.tile([P, PASSES, HALF], U32, name=f"pw{h}", align_bytes=64) for h in range(HALVES)]
         shift_plane = keep.tile([P, PASSES, N], U8, name="shift_plane", align_bytes=64)
@@ -186,9 +200,9 @@ def tile_spectral_unmix_rebuild_s10_kernel(
             src = pinv_words.rearrange("g p n t -> p g (n t)")[:, g0:g1, h * PACK * HALF : (h + 1) * PACK * HALF]
             nc.sync.dma_start(out=pinv_codes[h][:, g0:g1, :].bitcast(I32), in_=src.bitcast(I32))
 
-        def load_base(g):
-            src = base[g * K_PASS : (g + 1) * K_PASS, :].rearrange("(p j) n -> p j n", j=PACK)
-            nc.sync.dma_start(out=base_sb[g][:], in_=src)
+        def load_base(g, h):
+            src = base[g * K_PASS : (g + 1) * K_PASS, cols(h)].rearrange("(p j) n -> p j n", j=PACK)
+            nc.sync.dma_start(out=base_sb[g, h][:], in_=src)
 
         def zero(plane):
             nc.vector.memset(plane[:].rearrange("p g n -> p (g n)").bitcast(I32), 0)
@@ -198,12 +212,18 @@ def tile_spectral_unmix_rebuild_s10_kernel(
             for t in range(2):
                 for u in range(2):
                     out = bank[:, (2 * t + u) * P : (2 * t + u + 1) * P]
-                    nc.tensor.transpose(out, x_sorted[b][:, t, u, :], ident[:])
+                    if b in x_sorted:
+                        words = x_sorted[b][:, t, u, :]
+                    else:
+                        j, g = divmod(b, PASSES)
+                        words = x_pair[j][:, t, :].bitcast(F32)[:, 2 * P * g + u : 2 * P * (g + 1) : 2]
+                    nc.tensor.transpose(out, words, ident[:])
 
-        def copy(b):
+        def copy(b, engine="act"):
             woven = stage.tile([P, 2 * K_PASS], BF16, name="x_woven", align_bytes=64)
             x_woven[b] = woven
-            nc.scalar.copy(
+            move = nc.scalar.copy if engine == "act" else nc.vector.tensor_copy
+            move(
                 out=woven[:].bitcast(F32).rearrange("p (i r u) -> p i r u", i=2, u=2),
                 in_=banks["turn", b][:].rearrange("p (i u r) -> p i r u", i=2, u=2),
             )
@@ -229,7 +249,7 @@ def tile_spectral_unmix_rebuild_s10_kernel(
                 base_woven[g, h] = stage.tile([P, HALF, PACK], BF16, name="base_woven", align_bytes=64)
             span = slice(piece * PIECE, (piece + 1) * PIECE)
             out = base_woven[g, h][:, span, :].rearrange("p (c i) t -> p c t i", i=4)
-            src = base_sb[g][:, :, cols(h)][:, :, span].rearrange("p t (c i) -> p c t i", i=4)
+            src = base_sb[g, h][:, :, span].rearrange("p t (c i) -> p c t i", i=4)
             if engine == "act":
                 nc.scalar.copy(out=out, in_=src)
             else:
@@ -299,7 +319,7 @@ def tile_spectral_unmix_rebuild_s10_kernel(
             "zero_pinv": lambda: zero(pinv_plane),
             "ident": lambda: make_identity(nc, ident[:]),
             "load_shift_scales": lambda: load_scales(nc.scalar, shift_plane, shift_scales, 0),
-            "load_pinv_scales": lambda: load_scales(nc.sync, pinv_plane, pinv_scales, PINV_ROW),
+            "load_pinv_scales": lambda: load_scales(nc.gpsimd, pinv_plane, pinv_scales, PINV_ROW),
             "load_shift": load_shift,
             "load_pinv": load_pinv,
             "load_base": load_base,

@@ -31,23 +31,22 @@ PIECES = HALF // PIECE
 
 def schedule():
     s = []
-    s += [("load_first", 0), ("load_first", 1), ("load_first", 2), ("load_shift", 0)]
-    s += [("zero_shift",), ("zero_pinv",), ("ident",), ("load_shift_scales",), ("table",), ("load_eps",), ("load_pinv_scales",)]
-    s += [("load_pair", 1), ("load_base", 0, 0)] + [("load_pinv", 0, g, g + 1) for g in range(PASSES)]
-    s += [("load_pair", 2), ("load_pair", 3), ("load_base", 1, 0), ("load_base", 2, 0)]
+    s += [("load_first", 0), ("load_eps",), ("load_first", 1), ("load_first", 2), ("load_shift", 0)]
+    s += [("table",), ("zero_shift",), ("zero_pinv",), ("ident",), ("load_shift_scales",)]
+    s += [("load_pair", 1), ("load_pinv_scales",)] + [("load_pinv", 0, g, g + 1) for g in range(PASSES)] + [("load_pair", 2), ("load_base", 0, 0), ("load_pair", 3), ("load_base", 1, 0), ("load_base", 2, 0)]
     s += [("load_shift", 1), ("load_pinv", 1, 0, PASSES)] + [("load_base", g, 1) for g in range(PASSES)]
 
-    pieces = [("weave", g, h, i, "act") for h in range(HALVES) for g in range(PASSES) for i in range(PIECES)]
+    pieces = [("weave", g, h, i) for h in range(HALVES) for g in range(PASSES) for i in range(PIECES)]
     woven = []
     quantised = []
     to_mult = [(m, h) for h in range(HALVES) for m in range(TILES)]
     multiplied = []
     whole = (0, HALF)
 
-    def weave(n):
+    def weave(n, engine="act"):
         out = pieces[len(woven) : len(woven) + n]
         woven.extend(out)
-        return out
+        return [piece + (engine,) for piece in out]
 
     def quant_base():
         h, g = divmod(len(quantised), PASSES)
@@ -58,29 +57,27 @@ def schedule():
     def mult(n):
         out = to_mult[len(multiplied) : len(multiplied) + n]
         multiplied.extend(out)
-        return [("mult",) + tile for tile in out]
+        return [("mult",) + tile + ("dve",) for tile in out]
 
     def finish(part):
         return [("mm", "base") + part, ("final",) + part, ("store_rebuilt",) + part]
 
     s += [("sort", 0), ("sort", 1), ("sort", 2), ("turn", 0), ("turn", 1), ("turn", 2), ("turn_eps",)]
     s += [("copy", 0), ("copy", 1), ("quant", 0), ("copy", 2), ("quant", 1), ("quant", 2), ("copy_eps",)]
-    s += [("mm_both", "shift"), ("sort", 3), ("sort", 4), ("sort", 5)] + weave(2)
+    s += [("mm_both", "shift"), ("sort", 3), ("sort", 4), ("sort", 5)]
     s += [("turn", 3), ("turn", 4), ("turn", 5), ("add_eps", 0, 0), ("add_eps", 1, 0)]
-    s += [("copy", 3), ("copy", 4, "dve"), ("copy", 5), ("mm_both", "pinv")]
-    s += [("quant", 3), ("quant", 4), ("quant", 5), ("sort", 6), ("sort", 7), ("sort", 8)]
-    s += weave(1) + [("relu", 0, 0)]
+    s += [("copy", 3), ("copy", 4), ("copy", 5), ("mm_both", "pinv")]
+    s += [("quant", 3), ("quant", 4), ("quant", 5), ("relu", 0, 0)]
 
     for j in range(1, 4):
         a, b = 2 * j, 2 * j + 1
         t = 3 * (j + 1)
-        s += [("mm", "shift", a, 0), ("relu", a - 1, 0)] + weave(1)
-        s += mult([1,1,0][j - 1]) + [("add_eps", a, 0)] + mult([1,1,1][j - 1])
+        s += [("mm", "shift", a, 0), ("relu", a - 1, 0)] + weave([1,1,2][j - 1])
+        s += mult([1,2,1][j - 1]) + [("add_eps", a, 0)] + mult([1,0,1][j - 1]) + weave([0,2,2][j - 1], "dve")
         if j < 3:
             s += [("turn", t), ("turn", t + 1), ("turn", t + 2), ("copy", t), ("copy", t + 1), ("copy", t + 2)]
-            s += [("quant", t)] + ([("sort", 9)] if j == 1 else []) + [("quant", t + 1), ("quant", t + 2)]
-            s += [("sort", 10), ("sort", 11)] if j == 1 else []
-        s += [("mm", "pinv", a, 0), ("mm", "shift", b, 0), ("relu", a, 0)] + weave(1 if j < 3 else 2)
+            s += [("quant", t), ("quant", t + 1), ("quant", t + 2)]
+        s += [("mm", "pinv", a, 0), ("mm", "shift", b, 0), ("relu", a, 0)] + weave([1,1,1][j - 1])
         s += [("add_eps", b, 0), ("mm", "pinv", b, 0)]
         if j > 1:
             s += quant_base()
@@ -90,8 +87,8 @@ def schedule():
     prev = (TILES - 1, 0)
     for m in range(TILES):
         s += [("mm", "shift", m, 1), ("relu",) + prev, ("store_conc",) + prev]
-        s += weave([2,1,2,2,3,2,2,0][m]) + mult([1,1,1,2,1,1,1,1][m]) + [("add_eps", m, 1), ("mm", "pinv", m, 1)]
-        if m in [1,4,6,7]:
+        s += weave([1,2,2,2,2,2,2,0][m]) + mult([1,1,1,1,1,1,1,1][m]) + [("add_eps", m, 1), ("mm", "pinv", m, 1)]
+        if m in [1,3,5,7]:
             s += quant_base()
         prev = (m, 1)
         if m >= lag:
@@ -99,10 +96,8 @@ def schedule():
     rest = [(m, 0) + whole for m in range(TILES - lag, TILES)] + [(m, 1) + whole for m in range(TILES - 2)]
     rest += [(TILES - 2, 1, 0, 256), (TILES - 2, 1, 256, 256)]
     rest += [(TILES - 1, 1, 0, 256), (TILES - 1, 1, 256, 128), (TILES - 1, 1, 384, 128)]
-    s += [("relu",) + prev, ("store_conc",) + prev] + weave(PIECES)
+    s += [("relu",) + prev, ("store_conc",) + prev]
     for i, part in enumerate(rest):
-        if i == 99:
-            s += quant_base()
         s += finish(part)
         if i in [0,2]:
             s += mult(1)
@@ -295,8 +290,8 @@ def tile_spectral_unmix_rebuild_s10_kernel(
         def relu(m, h):
             nc.scalar.activation(out=conc[m, h][:], in_=banks["pinv", m, h, 0][:], func=ACT.Relu)
 
-        def mult(m, h):
-            nc.vector.tensor_tensor(out=work[m, h][:], in0=work[m, h][:], in1=conc[m, h][:], op=ALU.mult)
+        def mult(m, h, engine):
+            (nc.vector if engine == "dve" else nc.gpsimd).tensor_tensor(out=work[m, h][:], in0=work[m, h][:], in1=conc[m, h][:], op=ALU.mult)
 
         def final(m, h, first, width):
             part = work[m, h][:, first : first + width]
@@ -319,7 +314,7 @@ def tile_spectral_unmix_rebuild_s10_kernel(
             "zero_pinv": lambda: zero(pinv_plane),
             "ident": lambda: make_identity(nc, ident[:]),
             "load_shift_scales": lambda: load_scales(nc.scalar, shift_plane, shift_scales, 0),
-            "load_pinv_scales": lambda: load_scales(nc.gpsimd, pinv_plane, pinv_scales, PINV_ROW),
+            "load_pinv_scales": lambda: load_scales(nc.sync, pinv_plane, pinv_scales, PINV_ROW),
             "load_shift": load_shift,
             "load_pinv": load_pinv,
             "load_base": load_base,

@@ -24,16 +24,15 @@ TILES = M // P
 HALF = 512
 HALVES = N // HALF
 BANKS = 8
-PINV_ROW = 4
 PIECE = 128
 PIECES = HALF // PIECE
 
 
 def schedule():
     s = []
-    s += [("load_first", 0), ("load_eps",), ("load_first", 1), ("load_first", 2), ("load_shift", 0)]
-    s += [("table",), ("zero_shift",), ("zero_pinv",), ("ident",), ("load_shift_scales",)]
-    s += [("load_pair", 1), ("load_pinv_scales",)] + [("load_pinv", 0, g, g + 1) for g in range(PASSES)] + [("load_pair", 2), ("load_base", 0, 0), ("load_pair", 3), ("load_base", 1, 0), ("load_base", 2, 0)]
+    s += [("load_first", 0), ("load_eps",), ("load_first", 1), ("load_shift", 0)]
+    s += [("zero_shift",), ("seed",), ("zero_pinv",), ("ident",), ("load_shift_scales", 0), ("table",)]
+    s += [("load_pair", 1), ("load_pinv_scales", 0)] + [("load_pinv", 0, g, g + 1) for g in range(PASSES)] + [("load_pair", 2), ("load_base", 0, 0), ("load_pair", 3), ("load_base", 1, 0), ("load_shift_scales", 1), ("load_base", 2, 0), ("load_pinv_scales", 1)]
     s += [("load_shift", 1), ("load_pinv", 1, 0, PASSES)] + [("load_base", g, 1) for g in range(PASSES)]
 
     pieces = [("weave", g, h, i) for h in range(HALVES) for g in range(PASSES) for i in range(PIECES)]
@@ -62,45 +61,47 @@ def schedule():
     def finish(part):
         return [("mm", "base") + part, ("final",) + part, ("store_rebuilt",) + part]
 
-    s += [("sort", 0), ("sort", 1), ("sort", 2), ("turn", 0), ("turn", 1), ("turn", 2), ("turn_eps",)]
-    s += [("copy", 0), ("copy", 1), ("quant", 0), ("copy", 2), ("quant", 1), ("quant", 2), ("copy_eps",)]
+    s += [("turn_eps",), ("copy_eps",), ("sort", 0), ("sort", 1), ("sort", 2), ("turn", 0), ("turn", 1), ("turn", 2)]
+    s += [("copy", 0), ("copy", 1), ("quant", 0), ("copy", 2), ("quant", 1), ("quant", 2)]
     s += [("mm_both", "shift"), ("sort", 3), ("sort", 4), ("sort", 5)]
     s += [("turn", 3), ("turn", 4), ("turn", 5), ("add_eps", 0, 0), ("add_eps", 1, 0)]
     s += [("copy", 3), ("copy", 4), ("copy", 5), ("mm_both", "pinv")]
-    s += [("quant", 3), ("quant", 4), ("quant", 5), ("relu", 0, 0)]
+    s += [("quant", 3), ("quant", 4), ("quant", 5), ("sort", 6), ("sort", 7), ("sort", 8), ("relu", 0, 0)]
 
     for j in range(1, 4):
         a, b = 2 * j, 2 * j + 1
         t = 3 * (j + 1)
-        s += [("mm", "shift", a, 0), ("relu", a - 1, 0)] + weave([1,1,2][j - 1])
-        s += mult([1,2,1][j - 1]) + [("add_eps", a, 0)] + mult([1,0,1][j - 1]) + weave([0,2,2][j - 1], "dve")
+        s += [("mm", "shift", a, 0), ("relu", a - 1, 0)] + weave([1,1,1][j - 1])
+        s += mult([0,0,0][j - 1]) + [("add_eps", a, 0)] + mult([1,1,1][j - 1]) + weave([1,1,1][j - 1], "dve")
         if j < 3:
             s += [("turn", t), ("turn", t + 1), ("turn", t + 2), ("copy", t), ("copy", t + 1), ("copy", t + 2)]
-            s += [("quant", t), ("quant", t + 1), ("quant", t + 2)]
-        s += [("mm", "pinv", a, 0), ("mm", "shift", b, 0), ("relu", a, 0)] + weave([1,1,1][j - 1])
+            s += [("quant", t)] + ([("sort", 9)] if j == 1 else []) + [("quant", t + 1), ("quant", t + 2)]
+            s += [("sort", 10), ("sort", 11)] if j == 1 else []
+        s += [("mm", "pinv", a, 0), ("mm", "shift", b, 0), ("relu", a, 0)] + weave([1,2,2][j - 1])
         s += [("add_eps", b, 0), ("mm", "pinv", b, 0)]
         if j > 1:
             s += quant_base()
     for m in range(TILES - 1):
         s += [("store_conc", m, 0)]
-    lag = 3
+    parts = [(m, h) + whole for h in range(HALVES) for m in range(TILES)][:-2]
+    parts += [(TILES - 2, 1, 0, 256), (TILES - 2, 1, 256, 256)]
+    parts += [(TILES - 1, 1, 0, 256), (TILES - 1, 1, 256, 256)]
+    finished = []
     prev = (TILES - 1, 0)
     for m in range(TILES):
         s += [("mm", "shift", m, 1), ("relu",) + prev, ("store_conc",) + prev]
-        s += weave([1,2,2,2,2,2,2,0][m]) + mult([1,1,1,1,1,1,1,1][m]) + [("add_eps", m, 1), ("mm", "pinv", m, 1)]
+        s += weave([1,2,2,2,2,2,2,0][m]) + mult([1,1,2,2,2,2,1,1][m]) + [("add_eps", m, 1), ("mm", "pinv", m, 1)]
         if m in [1,3,5,7]:
             s += quant_base()
         prev = (m, 1)
-        if m >= lag:
-            s += finish((m - lag, 0) + whole)
-    rest = [(m, 0) + whole for m in range(TILES - lag, TILES)] + [(m, 1) + whole for m in range(TILES - 2)]
-    rest += [(TILES - 2, 1, 0, 256), (TILES - 2, 1, 256, 256)]
-    rest += [(TILES - 1, 1, 0, 256), (TILES - 1, 1, 256, 128), (TILES - 1, 1, 384, 128)]
+        for part in parts[len(finished) : len(finished) + [0,0,1,1,1,1,1,1][m]]:
+            s += finish(part)
+            finished.append(part)
     s += [("relu",) + prev, ("store_conc",) + prev]
-    for i, part in enumerate(rest):
-        s += finish(part)
-        if i in [0,2]:
+    for i, part in enumerate(parts[len(finished) :]):
+        if i in [1]:
             s += mult(1)
+        s += finish(part)
     assert len(woven) == len(pieces) and len(quantised) == PASSES * HALVES and len(multiplied) == 2 * TILES
     return s
 
@@ -116,7 +117,8 @@ def tile_spectral_unmix_rebuild_s10_kernel(
         ctx.enter_context(tc.manual_schedule())
 
         ident = keep.tile([P, P], F32, name="ident", align_bytes=64)
-        x_first = [keep.tile([P, 2, K_PASS], BF16, name=f"x0_{g}", align_bytes=64) for g in range(PASSES)]
+        x_first = keep.tile([P, 2, K_PASS], BF16, name="x_first", align_bytes=64)
+        x_rest = keep.tile([P, 2, K - K_PASS], BF16, name="x_rest", align_bytes=64)
         x_pair = {j: keep.tile([P, 2, K], BF16, name=f"x{j}", align_bytes=64) for j in range(1, TILES // 2)}
         scratch = keep.tile([P, 8], F32, name="scratch", align_bytes=64)
         seed = keep.tile([P, 8], F32, name="seed", align_bytes=64)
@@ -127,8 +129,8 @@ def tile_spectral_unmix_rebuild_s10_kernel(
                 base_sb[g, h] = keep.tile([P, PACK, HALF], BF16, name=f"base{g}_{h}", align_bytes=64)
         shift_codes = [keep.tile([P, PASSES, 2 * HALF], U8, name=f"sw{h}", align_bytes=64) for h in range(HALVES)]
         pinv_codes = [keep.tile([P, PASSES, HALF], U32, name=f"pw{h}", align_bytes=64) for h in range(HALVES)]
-        shift_plane = keep.tile([P, PASSES, N], U8, name="shift_plane", align_bytes=64)
-        pinv_plane = keep.tile([P, PASSES, N], U8, name="pinv_plane", align_bytes=64)
+        shift_plane = [keep.tile([P, PASSES, HALF], U8, name=f"shift_plane{h}", align_bytes=64) for h in range(HALVES)]
+        pinv_plane = [keep.tile([P, PASSES, HALF], U8, name=f"pinv_plane{h}", align_bytes=64) for h in range(HALVES)]
         base_codes = keep.tile([P, PASSES, N], U32, name="base_codes", align_bytes=64)
         base_plane = keep.tile([P, PASSES, N], U8, name="base_plane", align_bytes=64)
         x_codes = keep.tile([P, TILES * PASSES * P], U32, name="x_codes", align_bytes=64)
@@ -159,22 +161,26 @@ def tile_spectral_unmix_rebuild_s10_kernel(
             return slice(h * HALF, (h + 1) * HALF)
 
         def load_first(g):
-            src = spectra[0 : 2 * P, g * K_PASS : (g + 1) * K_PASS].rearrange("(t p) k -> p t k", p=P)
-            nc.sync.dma_start(out=x_first[g][:], in_=src)
+            src = spectra[0 : 2 * P, :].rearrange("(t p) k -> p t k", p=P)
+            if g == 0:
+                nc.sync.dma_start(out=x_first[:], in_=src[:, :, :K_PASS])
+            else:
+                nc.sync.dma_start(out=x_rest[:], in_=src[:, :, K_PASS:])
 
         def load_pair(j):
             src = spectra[2 * j * P : 2 * (j + 1) * P, :].rearrange("(t p) k -> p t k", p=P)
             nc.sync.dma_start(out=x_pair[j][:], in_=src)
 
         def table():
-            nc.vector.memset(seed[:], 0.0)
             nc.scalar.activation(out=scratch[:], in_=seed[:], func=ACT.Relu)
 
         def sort(b):
             j, g = divmod(b, PASSES)
             x_sorted[b] = stage.tile([P, 2, 2, P], F32, name="x_sorted", align_bytes=64)
-            if j == 0:
-                words = x_first[g][:].bitcast(F32)
+            if b == 0:
+                words = x_first[:].bitcast(F32)
+            elif j == 0:
+                words = x_rest[:].bitcast(F32)[:, :, 2 * P * (g - 1) : 2 * P * g]
             else:
                 words = x_pair[j][:].bitcast(F32)[:, :, 2 * P * g : 2 * P * (g + 1)]
             nc.vector.tensor_copy(out=x_sorted[b][:], in_=words.rearrange("p t (w u) -> p t u w", u=2))
@@ -182,10 +188,10 @@ def tile_spectral_unmix_rebuild_s10_kernel(
         def load_eps():
             nc.scalar.dma_start(out=eps_rows[:], in_=eps.rearrange("(p c) -> p c", p=P))
 
-        def load_scales(queue, plane, scales, first_row):
-            by_row = scales.rearrange("g (q r) n -> r q g n", r=4)
+        def load_scales(plane, scales, h, queue):
+            by_row = scales[:, :, cols(h)].rearrange("g (q r) n -> r q g n", r=4)
             for r in range(4):
-                queue.dma_start(out=plane[first_row + r : P : 32, :, :].bitcast(I32), in_=by_row[r].bitcast(I32))
+                queue.dma_start(out=plane[h][r:P:32, :, :].bitcast(I32), in_=by_row[r].bitcast(I32))
 
         def load_shift(h):
             src = shift_words.rearrange("g p c -> p g c")[:, :, h * 2 * HALF : (h + 1) * 2 * HALF]
@@ -200,7 +206,8 @@ def tile_spectral_unmix_rebuild_s10_kernel(
             nc.sync.dma_start(out=base_sb[g, h][:], in_=src)
 
         def zero(plane):
-            nc.vector.memset(plane[:].rearrange("p g n -> p (g n)").bitcast(I32), 0)
+            for h in range(HALVES):
+                nc.vector.memset(plane[h][:].rearrange("p g n -> p (g n)").bitcast(I32), 0)
 
         def turn(b):
             bank = new_bank(("turn", b))
@@ -268,9 +275,9 @@ def tile_spectral_unmix_rebuild_s10_kernel(
                 block = 2 * (PASSES * (m // 2) + g) + m % 2
                 span = slice(block * P, (block + 1) * P)
                 if which == "shift":
-                    rhs, rhs_scale = shift_codes[h][:, g, :].bitcast(FP4X4), shift_plane[:, g, cols(h)]
+                    rhs, rhs_scale = shift_codes[h][:, g, :].bitcast(FP4X4), shift_plane[h][:, g, :]
                 elif which == "pinv":
-                    rhs, rhs_scale = pinv_codes[h][:, g, :].bitcast(FP8X4), pinv_plane[PINV_ROW:, g, cols(h)]
+                    rhs, rhs_scale = pinv_codes[h][:, g, :].bitcast(FP8X4), pinv_plane[h][:, g, :]
                 else:
                     part = slice(h * HALF + first, h * HALF + first + width)
                     rhs, rhs_scale = base_codes[:, g, part].bitcast(FP8X4), base_plane[:, g, part]
@@ -308,13 +315,14 @@ def tile_spectral_unmix_rebuild_s10_kernel(
             "load_first": load_first,
             "load_pair": load_pair,
             "table": table,
+            "seed": lambda: nc.vector.memset(seed[:], 0.0),
             "sort": sort,
             "load_eps": load_eps,
             "zero_shift": lambda: zero(shift_plane),
             "zero_pinv": lambda: zero(pinv_plane),
             "ident": lambda: make_identity(nc, ident[:]),
-            "load_shift_scales": lambda: load_scales(nc.scalar, shift_plane, shift_scales, 0),
-            "load_pinv_scales": lambda: load_scales(nc.sync, pinv_plane, pinv_scales, PINV_ROW),
+            "load_shift_scales": lambda h: load_scales(shift_plane, shift_scales, h, nc.scalar if h == 0 else nc.sync),
+            "load_pinv_scales": lambda h: load_scales(pinv_plane, pinv_scales, h, nc.sync),
             "load_shift": load_shift,
             "load_pinv": load_pinv,
             "load_base": load_base,

@@ -32,7 +32,7 @@ def schedule():
     s = []
     s += [("load_first", 0), ("load_eps",), ("load_first", 1), ("load_shift", 0)]
     s += [("zero_shift",), ("seed",), ("zero_pinv",), ("ident",), ("load_shift_scales", 0), ("table",)]
-    s += [("load_pair", 1), ("load_pinv_scales", 0)] + [("load_pinv", 0, g, g + 1) for g in range(PASSES)] + [("load_pair", 2), ("load_base", 0, 0), ("load_pair", 3), ("load_base", 1, 0), ("load_shift_scales", 1), ("load_base", 2, 0), ("load_pinv_scales", 1)]
+    s += [("load_pair", 1), ("load_pinv_scales", 0)] + [("load_pinv", 0, g, g + 1) for g in range(PASSES)] + [("load_pair", 2), ("load_pair", 3), ("load_base", 0, 0), ("load_base", 1, 0), ("load_shift_scales", 1), ("load_base", 2, 0), ("load_pinv_scales", 1)]
     s += [("load_shift", 1), ("load_pinv", 1, 0, PASSES)] + [("load_base", g, 1) for g in range(PASSES)]
 
     pieces = [("weave", g, h, i) for h in range(HALVES) for g in range(PASSES) for i in range(PIECES)]
@@ -71,13 +71,19 @@ def schedule():
     for j in range(1, 4):
         a, b = 2 * j, 2 * j + 1
         t = 3 * (j + 1)
-        s += [("mm", "shift", a, 0), ("relu", a - 1, 0)] + weave([1,1,1][j - 1])
-        s += mult([0,0,0][j - 1]) + [("add_eps", a, 0)] + mult([1,1,1][j - 1]) + weave([1,1,1][j - 1], "dve")
+        s += [("mm", "shift", a, 0), ("relu", a - 1, 0)] + weave([0,1,2][j - 1])
+        s += mult([0,0,1][j - 1]) + [("add_eps", a, 0)] + mult([1,1,1][j - 1]) + weave([0,1,2][j - 1], "dve")
+        if j == 1:
+            s += [("mm", "pinv", a, 0), ("relu", a, 0)]
         if j < 3:
             s += [("turn", t), ("turn", t + 1), ("turn", t + 2), ("copy", t), ("copy", t + 1), ("copy", t + 2)]
             s += [("quant", t)] + ([("sort", 9)] if j == 1 else []) + [("quant", t + 1), ("quant", t + 2)]
             s += [("sort", 10), ("sort", 11)] if j == 1 else []
-        s += [("mm", "pinv", a, 0), ("mm", "shift", b, 0), ("relu", a, 0)] + weave([1,2,2][j - 1])
+        if j == 1:
+            s += [("mm", "shift", b, 0)]
+        else:
+            s += [("mm", "pinv", a, 0), ("mm", "shift", b, 0), ("relu", a, 0)]
+        s += weave([1,1,2][j - 1])
         s += [("add_eps", b, 0), ("mm", "pinv", b, 0)]
         if j > 1:
             s += quant_base()
@@ -90,16 +96,16 @@ def schedule():
     prev = (TILES - 1, 0)
     for m in range(TILES):
         s += [("mm", "shift", m, 1), ("relu",) + prev, ("store_conc",) + prev]
-        s += weave([1,2,2,2,2,2,2,0][m]) + mult([1,1,2,2,2,2,1,1][m]) + [("add_eps", m, 1), ("mm", "pinv", m, 1)]
-        if m in [1,3,5,7]:
+        s += weave([2,2,2,2,2,2,2,0][m]) + mult([1,1,1,2,1,1,1,1][m]) + [("add_eps", m, 1), ("mm", "pinv", m, 1)]
+        if m in [1,4,6,7]:
             s += quant_base()
         prev = (m, 1)
-        for part in parts[len(finished) : len(finished) + [0,0,1,1,1,1,1,1][m]]:
+        for part in parts[len(finished) : len(finished) + [0,0,0,1,1,1,1,1][m]]:
             s += finish(part)
             finished.append(part)
     s += [("relu",) + prev, ("store_conc",) + prev]
     for i, part in enumerate(parts[len(finished) :]):
-        if i in [1]:
+        if i in [0,2,4]:
             s += mult(1)
         s += finish(part)
     assert len(woven) == len(pieces) and len(quantised) == PASSES * HALVES and len(multiplied) == 2 * TILES

from contextlib import ExitStack

import concourse.mybir as mybir
from concourse.masks import make_identity

M, K, N = 1024, 1536, 1024
FLOPS = 3 * 2 * M * K * N

F32 = mybir.dt.float32
BF16 = mybir.dt.bfloat16
I32 = mybir.dt.int32
U32 = mybir.dt.uint32
U8 = mybir.dt.uint8
FP8X4 = mybir.dt.float8_e4m3fn_x4
FP4X4 = mybir.dt.float4_e2m1fn_x4
ALU = mybir.AluOpType
ACT = mybir.ActivationFunctionType

P = 128
PACK = 4
K_PASS = P * PACK
PASSES = K // K_PASS
TILES = M // P
HALF = 512
HALVES = N // HALF
BANKS = 8
PIECE = 128
PIECES = HALF // PIECE


def schedule():
    s = []
    s += [("load_first", 0), ("load_eps",), ("load_first", 1), ("load_shift", 0)]
    s += [("zero_shift",), ("seed",), ("zero_pinv",), ("ident",), ("load_shift_scales", 0), ("table",)]
    s += [("load_pair", 1), ("load_pinv_scales", 0)] + [("load_pinv", 0, g, g + 1) for g in range(PASSES)] + [("load_pair", 2), ("load_pair", 3), ("load_base", 0, 0), ("load_base", 1, 0), ("load_shift_scales", 1), ("load_base", 2, 0), ("load_pinv_scales", 1)]
    s += [("load_shift", 1), ("load_pinv", 1, 0, PASSES)] + [("load_base", g, 1) for g in range(PASSES)]

    pieces = [("weave", g, h, i) for h in range(HALVES) for g in range(PASSES) for i in range(PIECES)]
    woven = []
    quantised = []
    to_mult = [(m, h) for h in range(HALVES) for m in range(TILES)]
    multiplied = []
    whole = (0, HALF)

    def weave(n, engine="act"):
        out = pieces[len(woven) : len(woven) + n]
        woven.extend(out)
        return [piece + (engine,) for piece in out]

    def quant_base():
        h, g = divmod(len(quantised), PASSES)
        quantised.append((g, h))
        assert len(woven) >= PIECES * len(quantised)
        return [("quant_base", g, h)]

    def mult(n):
        out = to_mult[len(multiplied) : len(multiplied) + n]
        multiplied.extend(out)
        return [("mult",) + tile + ("dve",) for tile in out]

    def finish(part):
        return [("mm", "base") + part, ("final",) + part, ("store_rebuilt",) + part]

    s += [("turn_eps",), ("copy_eps",), ("sort", 0), ("sort", 1), ("sort", 2), ("turn", 0), ("turn", 1), ("turn", 2)]
    s += [("copy", 0), ("copy", 1), ("quant", 0), ("copy", 2), ("quant", 1), ("quant", 2)]
    s += [("mm_both", "shift"), ("sort", 3), ("sort", 4), ("sort", 5)]
    s += [("turn", 3), ("turn", 4), ("turn", 5), ("add_eps", 0, 0), ("add_eps", 1, 0)]
    s += [("copy", 3), ("copy", 4), ("copy", 5), ("mm_both", "pinv")]
    s += [("quant", 3), ("quant", 4), ("quant", 5), ("sort", 6), ("sort", 7), ("sort", 8), ("relu", 0, 0)]

    for j in range(1, 4):
        a, b = 2 * j, 2 * j + 1
        t = 3 * (j + 1)
        s += [("mm", "shift", a, 0), ("relu", a - 1, 0)] + weave([0,1,2][j - 1])
        s += mult([0,0,1][j - 1]) + [("add_eps", a, 0)] + mult([1,1,1][j - 1]) + weave([0,1,2][j - 1], "dve")
        if j == 1:
            s += [("mm", "pinv", a, 0), ("relu", a, 0)]
        if j < 3:
            s += [("turn", t), ("turn", t + 1), ("turn", t + 2), ("copy", t), ("copy", t + 1), ("copy", t + 2)]
            s += [("quant", t)] + ([("sort", 9)] if j == 1 else []) + [("quant", t + 1), ("quant", t + 2)]
            s += [("sort", 10), ("sort", 11)] if j == 1 else []
        if j == 1:
            s += [("mm", "shift", b, 0)]
        else:
            s += [("mm", "pinv", a, 0), ("mm", "shift", b, 0), ("relu", a, 0)]
        s += weave([1,1,2][j - 1])
        s += [("add_eps", b, 0), ("mm", "pinv", b, 0)]
        if j > 1:
            s += quant_base()
    for m in range(TILES - 1):
        s += [("store_conc", m, 0)]
    parts = [(m, h) + whole for h in range(HALVES) for m in range(TILES)][:-2]
    parts += [(TILES - 2, 1, 0, 256), (TILES - 2, 1, 256, 256)]
    parts += [(TILES - 1, 1, 0, 256), (TILES - 1, 1, 256, 256)]
    finished = []
    prev = (TILES - 1, 0)
    for m in range(TILES):
        s += [("mm", "shift", m, 1), ("relu",) + prev, ("store_conc",) + prev]
        s += weave([2,2,2,2,2,2,2,0][m]) + mult([1,1,1,2,1,1,1,1][m]) + [("add_eps", m, 1), ("mm", "pinv", m, 1)]
        if m in [1,4,6,7]:
            s += quant_base()
        prev = (m, 1)
        for part in parts[len(finished) : len(finished) + [0,0,0,1,1,1,1,1][m]]:
            s += finish(part)
            finished.append(part)
    s += [("relu",) + prev, ("store_conc",) + prev]
    for i, part in enumerate(parts[len(finished) :]):
        if i in [0,2,4]:
            s += mult(1)
        s += finish(part)
    assert len(woven) == len(pieces) and len(quantised) == PASSES * HALVES and len(multiplied) == 2 * TILES
    return s


def tile_spectral_unmix_rebuild_s10_kernel(
    tc, spectra, shift_words, shift_scales, pinv_words, pinv_scales, base, eps, conc_out, rebuilt_out
):
    nc = tc.nc
    with ExitStack() as ctx:
        keep = ctx.enter_context(tc.tile_pool(name="keep", bufs=1))
        stage = ctx.enter_context(tc.tile_pool(name="stage", bufs=4))
        psum = ctx.enter_context(tc.psum_pool(name="psum", bufs=1))
        ctx.enter_context(tc.manual_schedule())

        ident = keep.tile([P, P], F32, name="ident", align_bytes=64)
        x_first = keep.tile([P, 2, K_PASS], BF16, name="x_first", align_bytes=64)
        x_rest = keep.tile([P, 2, K - K_PASS], BF16, name="x_rest", align_bytes=64)
        x_pair = {j: keep.tile([P, 2, K], BF16, name=f"x{j}", align_bytes=64) for j in range(1, TILES // 2)}
        scratch = keep.tile([P, 8], F32, name="scratch", align_bytes=64)
        seed = keep.tile([P, 8], F32, name="seed", align_bytes=64)
        x_sorted = {}
        base_sb = {}
        for g in range(PASSES):
            for h in range(HALVES):
                base_sb[g, h] = keep.tile([P, PACK, HALF], BF16, name=f"base{g}_{h}", align_bytes=64)
        shift_codes = [keep.tile([P, PASSES, 2 * HALF], U8, name=f"sw{h}", align_bytes=64) for h in range(HALVES)]
        pinv_codes = [keep.tile([P, PASSES, HALF], U32, name=f"pw{h}", align_bytes=64) for h in range(HALVES)]
        shift_plane = [keep.tile([P, PASSES, HALF], U8, name=f"shift_plane{h}", align_bytes=64) for h in range(HALVES)]
        pinv_plane = [keep.tile([P, PASSES, HALF], U8, name=f"pinv_plane{h}", align_bytes=64) for h in range(HALVES)]
        base_codes = keep.tile([P, PASSES, N], U32, name="base_codes", align_bytes=64)
        base_plane = keep.tile([P, PASSES, N], U8, name="base_plane", align_bytes=64)
        x_codes = keep.tile([P, TILES * PASSES * P], U32, name="x_codes", align_bytes=64)
        x_plane = keep.tile([P, TILES * PASSES * P], U8, name="x_plane", align_bytes=64)
        eps_rows = keep.tile([P, N // P], BF16, name="eps_rows", align_bytes=64)
        eps_all = keep.tile([P, N], BF16, name="eps_all", align_bytes=64)
        conc = {}
        work = {}
        for m in range(TILES):
            for h in range(HALVES):
                conc[m, h] = keep.tile([P, HALF], F32, name=f"conc{m}_{h}", align_bytes=64)
                work[m, h] = keep.tile([P, HALF], F32, name=f"work{m}_{h}", align_bytes=64)

        banks = {}
        x_woven = {}
        base_woven = {}
        taken = []

        def new_bank(key):
            banks[key] = psum.tile([P, HALF], F32, name=f"bank{len(taken) % BANKS}")
            taken.append(key)
            return banks[key]

        def rows(m):
            return slice(m * P, (m + 1) * P)

        def cols(h):
            return slice(h * HALF, (h + 1) * HALF)

        def load_first(g):
            src = spectra[0 : 2 * P, :].rearrange("(t p) k -> p t k", p=P)
            if g == 0:
                nc.sync.dma_start(out=x_first[:], in_=src[:, :, :K_PASS])
            else:
                nc.sync.dma_start(out=x_rest[:], in_=src[:, :, K_PASS:])

        def load_pair(j):
            src = spectra[2 * j * P : 2 * (j + 1) * P, :].rearrange("(t p) k -> p t k", p=P)
            nc.sync.dma_start(out=x_pair[j][:], in_=src)

        def table():
            nc.scalar.activation(out=scratch[:], in_=seed[:], func=ACT.Relu)

        def sort(b):
            j, g = divmod(b, PASSES)
            x_sorted[b] = stage.tile([P, 2, 2, P], F32, name="x_sorted", align_bytes=64)
            if b == 0:
                words = x_first[:].bitcast(F32)
            elif j == 0:
                words = x_rest[:].bitcast(F32)[:, :, 2 * P * (g - 1) : 2 * P * g]
            else:
                words = x_pair[j][:].bitcast(F32)[:, :, 2 * P * g : 2 * P * (g + 1)]
            nc.vector.tensor_copy(out=x_sorted[b][:], in_=words.rearrange("p t (w u) -> p t u w", u=2))

        def load_eps():
            nc.scalar.dma_start(out=eps_rows[:], in_=eps.rearrange("(p c) -> p c", p=P))

        def load_scales(plane, scales, h, queue):
            by_row = scales[:, :, cols(h)].rearrange("g (q r) n -> r q g n", r=4)
            for r in range(4):
                queue.dma_start(out=plane[h][r:P:32, :, :].bitcast(I32), in_=by_row[r].bitcast(I32))

        def load_shift(h):
            src = shift_words.rearrange("g p c -> p g c")[:, :, h * 2 * HALF : (h + 1) * 2 * HALF]
            nc.sync.dma_start(out=shift_codes[h][:].bitcast(I32), in_=src.bitcast(I32))

        def load_pinv(h, g0, g1):
            src = pinv_words.rearrange("g p n t -> p g (n t)")[:, g0:g1, h * PACK * HALF : (h + 1) * PACK * HALF]
            nc.sync.dma_start(out=pinv_codes[h][:, g0:g1, :].bitcast(I32), in_=src.bitcast(I32))

        def load_base(g, h):
            src = base[g * K_PASS : (g + 1) * K_PASS, cols(h)].rearrange("(p j) n -> p j n", j=PACK)
            nc.sync.dma_start(out=base_sb[g, h][:], in_=src)

        def zero(plane):
            for h in range(HALVES):
                nc.vector.memset(plane[h][:].rearrange("p g n -> p (g n)").bitcast(I32), 0)

        def turn(b):
            bank = new_bank(("turn", b))
            for t in range(2):
                for u in range(2):
                    out = bank[:, (2 * t + u) * P : (2 * t + u + 1) * P]
                    if b in x_sorted:
                        words = x_sorted[b][:, t, u, :]
                    else:
                        j, g = divmod(b, PASSES)
                        words = x_pair[j][:, t, :].bitcast(F32)[:, 2 * P * g + u : 2 * P * (g + 1) : 2]
                    nc.tensor.transpose(out, words, ident[:])

        def copy(b, engine="act"):
            woven = stage.tile([P, 2 * K_PASS], BF16, name="x_woven", align_bytes=64)
            x_woven[b] = woven
            move = nc.scalar.copy if engine == "act" else nc.vector.tensor_copy
            move(
                out=woven[:].bitcast(F32).rearrange("p (i r u) -> p i r u", i=2, u=2),
                in_=banks["turn", b][:].rearrange("p (i u r) -> p i r u", i=2, u=2),
            )

        def quant(b):
            span = slice(2 * b * P, 2 * (b + 1) * P)
            nc.vector.quantize_mx(out=x_codes[:, span].bitcast(FP8X4), scales=x_plane[:, span], in_=x_woven[b][:])

        def turn_eps():
            bank = new_bank("eps")
            words = eps_rows[:].bitcast(F32)
            for c in range(4):
                nc.tensor.transpose(bank[:, c * P : (c + 1) * P], words[:, c : c + 1].to_broadcast([P, P]), ident[:])

        def copy_eps():
            nc.scalar.copy(
                out=eps_all[:].bitcast(F32).rearrange("p (n c) -> p n c", c=4),
                in_=banks["eps"][:].rearrange("p (c n) -> p n c", c=4),
            )

        def weave(g, h, piece, engine):
            if piece == 0:
                base_woven[g, h] = stage.tile([P, HALF, PACK], BF16, name="base_woven", align_bytes=64)
            span = slice(piece * PIECE, (piece + 1) * PIECE)
            out = base_woven[g, h][:, span, :].rearrange("p (c i) t -> p c t i", i=4)
            src = base_sb[g, h][:, :, span].rearrange("p t (c i) -> p c t i", i=4)
            if engine == "act":
                nc.scalar.copy(out=out, in_=src)
            else:
                nc.vector.tensor_copy(out=out, in_=src)

        def quant_base(g, h):
            nc.vector.quantize_mx(
                out=base_codes[:, g, cols(h)].bitcast(FP8X4),
                scales=base_plane[:, g, cols(h)],
                in_=base_woven[g, h][:].rearrange("p n t -> p (n t)"),
            )

        def mm_both(which):
            for g in range(PASSES):
                for m in range(2):
                    mm(which, m, 0, passes=[g])

        def mm(which, m, h, first=0, width=HALF, passes=range(PASSES)):
            for g in passes:
                bank = new_bank((which, m, h, first)) if g == 0 else banks[which, m, h, first]
                block = 2 * (PASSES * (m // 2) + g) + m % 2
                span = slice(block * P, (block + 1) * P)
                if which == "shift":
                    rhs, rhs_scale = shift_codes[h][:, g, :].bitcast(FP4X4), shift_plane[h][:, g, :]
                elif which == "pinv":
                    rhs, rhs_scale = pinv_codes[h][:, g, :].bitcast(FP8X4), pinv_plane[h][:, g, :]
                else:
                    part = slice(h * HALF + first, h * HALF + first + width)
                    rhs, rhs_scale = base_codes[:, g, part].bitcast(FP8X4), base_plane[:, g, part]
                nc.tensor.matmul_mx(
                    out=bank[:, :width],
                    lhsT=x_codes[:, span].bitcast(FP8X4),
                    lhsT_scale=x_plane[:, span],
                    rhs=rhs,
                    rhs_scale=rhs_scale,
                    start=(g == 0),
                    stop=(g == PASSES - 1),
                )

        def add_eps(m, h):
            nc.vector.tensor_tensor(out=work[m, h][:], in0=banks["shift", m, h, 0][:], in1=eps_all[:, cols(h)], op=ALU.add)

        def relu(m, h):
            nc.scalar.activation(out=conc[m, h][:], in_=banks["pinv", m, h, 0][:], func=ACT.Relu)

        def mult(m, h, engine):
            (nc.vector if engine == "dve" else nc.gpsimd).tensor_tensor(out=work[m, h][:], in0=work[m, h][:], in1=conc[m, h][:], op=ALU.mult)

        def final(m, h, first, width):
            part = work[m, h][:, first : first + width]
            nc.vector.tensor_tensor(out=part, in0=banks["base", m, h, first][:, :width], in1=part, op=ALU.add)

        def store_conc(m, h):
            nc.sync.dma_start(out=conc_out[rows(m), cols(h)], in_=conc[m, h][:])

        def store_rebuilt(m, h, first, width):
            part = slice(h * HALF + first, h * HALF + first + width)
            nc.sync.dma_start(out=rebuilt_out[rows(m), part], in_=work[m, h][:, first : first + width])

        steps = {
            "load_first": load_first,
            "load_pair": load_pair,
            "table": table,
            "seed": lambda: nc.vector.memset(seed[:], 0.0),
            "sort": sort,
            "load_eps": load_eps,
            "zero_shift": lambda: zero(shift_plane),
            "zero_pinv": lambda: zero(pinv_plane),
            "ident": lambda: make_identity(nc, ident[:]),
            "load_shift_scales": lambda h: load_scales(shift_plane, shift_scales, h, nc.scalar if h == 0 else nc.sync),
            "load_pinv_scales": lambda h: load_scales(pinv_plane, pinv_scales, h, nc.sync),
            "load_shift": load_shift,
            "load_pinv": load_pinv,
            "load_base": load_base,
            "turn": turn,
            "copy": copy,
            "quant": quant,
            "turn_eps": turn_eps,
            "copy_eps": copy_eps,
            "weave": weave,
            "quant_base": quant_base,
            "mm": mm,
            "mm_both": mm_both,
            "add_eps": add_eps,
            "relu": relu,
            "mult": mult,
            "final": final,
            "store_conc": store_conc,
            "store_rebuilt": store_rebuilt,
        }
        for step in schedule():
            steps[step[0]](*step[1:])
